import numpy as np
import ml_dtypes


def mxq(x, axis, fmt="e4m3"):
    dtype, down = {"e4m3": (ml_dtypes.float8_e4m3fn, 7), "e5m2": (ml_dtypes.float8_e5m2, 14)}[fmt]
    v = np.moveaxis(np.asarray(x, np.float32).astype(ml_dtypes.bfloat16).astype(np.float64), axis, -1)
    blocks = v.reshape(v.shape[:-1] + (-1, 32))
    amax = np.abs(blocks).max(-1, keepdims=True)
    byte = np.maximum(np.where(amax > 0, np.frexp(amax)[1] - 1 + 127, 0) - down, 1)
    scale = np.exp2(byte - 127.0)
    codes = (blocks / scale).astype(np.float32).astype(dtype).astype(np.float64)
    return np.moveaxis((codes * scale).reshape(v.shape), -1, axis)


WIDE = False


def mx_kscale(k):
    if not WIDE:
        return np.ones(k)
    levels = np.array([10, -10, 5, -5, 0])
    if k % 512:
        return np.exp2(np.random.permutation(np.resize(levels, k // 32))).repeat(32)
    a = np.empty((k // 512, 16))
    for p in range(k // 512):
        a[p, :8] = np.random.permutation(np.resize(levels, 8))
        for g in range(8):
            far = levels[np.abs(levels - a[p, g]) >= 10]
            a[p, g + 8] = far[np.random.randint(len(far))]
    return np.exp2(a.ravel()).repeat(32)


def f64(x):
    return np.asarray(x).astype(np.float64)


def striped(idx):
    return np.tile(np.asarray(idx).reshape(-1, 16).T, (8, 1)).astype(np.uint16)


def unstriped(offs):
    return offs[:16].T.reshape(-1).astype(np.int64)


E2M1 = np.array([0.0, 0.5, 1.0, 1.5, 2.0, 3.0, 4.0, 6.0, -0.0, -0.5, -1.0, -1.5, -2.0, -3.0, -4.0, -6.0])


def pack_weight(w, fmt):
    k, n = w.shape
    w = f64(np.asarray(w, np.float32).astype(ml_dtypes.bfloat16)).reshape(k // 32, 32, n)
    amax = np.abs(w).max(1)
    if fmt == "e4m3":
        byte = np.frexp(amax)[1] - 1 + 127 - 7
    else:
        mant, ex = np.frexp(amax / 6.0)
        byte = np.where(mant > 0.5, ex, ex - 1) + 127
    byte = np.clip(np.where(amax > 0, byte, 1), 1, 254)
    scaled = (w * np.exp2(127.0 - byte)[:, None, :]).reshape(k, n).astype(np.float32)
    by_word = np.ascontiguousarray(scaled.reshape(k // 512, 128, 4, n).transpose(0, 1, 3, 2))
    if fmt == "e4m3":
        words = by_word.astype(ml_dtypes.float8_e4m3fn).view(np.uint8)
    else:
        c = by_word.astype(ml_dtypes.float4_e2m1fn).view(np.uint8) & 0xF
        words = (c[..., 0::2] | (c[..., 1::2] << 4)).reshape(k // 512, 128, 2 * n)
    return np.ascontiguousarray(words), np.ascontiguousarray(byte.astype(np.uint8).reshape(k // 512, 16, n))


def unpack_weight(words, scales, fmt):
    g, _, n = scales.shape
    words = np.ascontiguousarray(words).reshape(g, 128, n, -1)
    if fmt == "e4m3":
        vals = words.view(ml_dtypes.float8_e4m3fn).astype(np.float64)
    else:
        nib = np.empty((g, 128, n, 4), np.uint8)
        nib[..., 0::2] = words & 0xF
        nib[..., 1::2] = words >> 4
        vals = E2M1[nib]
    vals = vals * np.repeat(np.exp2(scales.astype(np.float64) - 127.0), 8, axis=1)[..., None]
    return vals.transpose(0, 1, 3, 2).reshape(g * 512, n)


K, T, J, I, N = 1024, 1024, 512, 512, 512


def setup_inputs():
    n = np.random.standard_normal
    idx = np.random.permutation(T)[:J]
    idx2 = np.random.permutation(T)[:I]
    fk = mx_kscale(K)
    xtp = pack_weight(n((K, T)) / fk[:, None], "e4m3")
    wap = pack_weight(n((K, N)) * 1 / np.sqrt(K) * fk[:, None], "e2m1")
    return {
        "xt_words": xtp[0],
        "xt_scales": xtp[1],
        "wa_words": wap[0],
        "wa_scales": wap[1],
        "wb": (n((K, N)) * 1 / np.sqrt(K) * fk[:, None]).astype(np.float32),
        "gb": (np.random.uniform(0.4, 1.2, (1, I))).astype(np.float32),
        "res": (1.0 * n((N, T))).astype(np.float32),
        "offs": striped(idx),
        "offs2": striped(idx2),
    }


def reference(xt_words, xt_scales, wa_words, wa_scales, wb, gb, res, offs, offs2):
    idx = unstriped(offs)
    idx2 = unstriped(offs2)
    xtu = unpack_weight(xt_words, xt_scales, "e4m3")
    wau = unpack_weight(wa_words, wa_scales, "e2m1")
    xtidxg = xtu[:, idx]
    p = wau.T @ xtidxg
    wbq = mxq(f64(wb), 0, "e4m3")
    xtidx2g = xtu[:, idx2]
    q = wbq.T @ xtidx2g
    qw = q * f64(gb)
    pg = np.zeros((N, T))
    pg[:, idx] = p
    qg = np.zeros((N, T))
    qg[:, idx2] = qw
    y = pg + qg * np.exp(0.0 - np.abs(pg)) + 0.3 * f64(res)
    return y

@@ -1,0 +1,229 @@
+from contextlib import ExitStack
+
+import concourse.mybir as mybir
+from concourse.masks import make_identity
+
+K, T, J, N = 1024, 1024, 512, 512
+FLOPS = 2 * 2 * K * J * N
+
+F32 = mybir.dt.float32
+BF16 = mybir.dt.bfloat16
+I32 = mybir.dt.int32
+U32 = mybir.dt.uint32
+U16 = mybir.dt.uint16
+U8 = mybir.dt.uint8
+FP8X4 = mybir.dt.float8_e4m3fn_x4
+FP4X4 = mybir.dt.float4_e2m1fn_x4
+ACT = mybir.ActivationFunctionType
+ALU = mybir.AluOpType
+
+P = 128
+PASSES = K // 512
+BLOCKS = N // P
+BANK = 512
+HALVES = T // BANK
+CHUNKS = BANK // P
+RES_SCALE = 0.3
+
+
+def tile_moe_second_choice_where_first_is_weak_kernel(
+    tc, xt_words, xt_scales, wa_words, wa_scales, wb, gb, res, offs, offs2, out
+):
+    nc = tc.nc
+    with ExitStack() as ctx:
+        keep = ctx.enter_context(tc.tile_pool(name="keep", bufs=1))
+        ring = ctx.enter_context(tc.tile_pool(name="ring", bufs=2))
+        psum = ctx.enter_context(tc.psum_pool(name="psum", bufs=1))
+
+        def held(name, shape, dtype):
+            return keep.tile(shape, dtype, name=name, align_bytes=64)
+
+        list_a = held("list_a", [P, J // 16], U16)
+        list_b = held("list_b", [P, J // 16], U16)
+        x_words = [held("x_words%d" % z, [P, T], U32) for z in range(PASSES)]
+        x_scales_a = held("x_scales_a", [P, PASSES, T], U8)
+        x_scales_b = held("x_scales_b", [P, T], U8)
+        wa_codes = held("wa_codes", [P, PASSES, 2 * N], U8)
+        wa_plane = held("wa_plane", [P, PASSES, N], U8)
+        wb_raw = [held("wb_raw%d" % z, [P, 4 * N], F32) for z in range(PASSES)]
+        gb_rows = held("gb_rows", [P, J], F32)
+        res_sb = [held("res%d" % b, [P, T], F32) for b in range(BLOCKS)]
+        p_win = [held("p_win%d" % i, [P, T], F32) for i in range(2)]
+        q_win = held("q_win", [P, T], F32)
+        ident = held("ident", [P, P], F32)
+
+        nc.vector.memset(x_scales_a[:].rearrange("p z t -> p (z t)").bitcast(I32), 0)
+        nc.vector.memset(wa_plane[:].rearrange("p z n -> p (z n)").bitcast(I32), 0)
+        nc.vector.memset(x_scales_b[:].bitcast(I32), 0)
+        for win in p_win + [q_win]:
+            nc.vector.memset(win[:], 0.0)
+        make_identity(nc, ident[:])
+
+        xs_i32 = xt_scales.bitcast(I32)
+        was_i32 = wa_scales.bitcast(I32)
+
+        nc.sync.dma_start(list_a[:], offs)
+        nc.sync.dma_start(x_words[0][:].bitcast(I32), xt_words[0].rearrange("p c r -> p (c r)").bitcast(I32))
+        nc.sync.dma_start(x_words[1][:].bitcast(I32), xt_words[1].rearrange("p c r -> p (c r)").bitcast(I32))
+        for r in range(4):
+            nc.sync.dma_start(
+                x_scales_a[r:P:32, :, :].bitcast(I32), xs_i32[:, r:16:4, :].rearrange("z q c -> q z c")
+            )
+        nc.sync.dma_start(wa_codes[:].bitcast(I32), wa_words.bitcast(I32).rearrange("z p c -> p z c"))
+        for r in range(4):
+            nc.sync.dma_start(
+                wa_plane[r:P:32, :, :].bitcast(I32), was_i32[:, r:16:4, :].rearrange("z q c -> q z c")
+            )
+        nc.sync.dma_start(list_b[:], offs2)
+        for q in range(4):
+            nc.sync.dma_start(x_scales_b[32 * q : 32 * q + 8, :].bitcast(I32), xs_i32[:, 4 * q : 4 * q + 4, :])
+        for z in range(PASSES):
+            nc.sync.dma_start(wb_raw[z][:], wb[512 * z : 512 * (z + 1), :].rearrange("(p j) n -> p (j n)", j=4))
+        nc.sync.dma_start(gb_rows[:], gb[0].partition_broadcast(P))
+        for b in range(BLOCKS):
+            nc.sync.dma_start(res_sb[b][:], res[b * P : (b + 1) * P, :])
+
+        a_words = [held("a_words%d" % z, [P, J], U32) for z in range(PASSES)]
+        a_plane = [held("a_plane%d" % z, [P, J], U8) for z in range(PASSES)]
+        b_words = [held("b_words%d" % z, [P, J], U32) for z in range(PASSES)]
+        b_plane = held("b_plane", [P, J], U8)
+        for z in range(PASSES):
+            nc.vector.tensor_copy(a_words[z][:], x_words[z][:].indirect(list_a[:]))
+        for z in range(PASSES):
+            nc.vector.tensor_copy(a_plane[z][:], x_scales_a[:, z, :].indirect(list_a[:]))
+        for z in range(PASSES):
+            nc.vector.tensor_copy(b_words[z][:], x_words[z][:].indirect(list_b[:]))
+        nc.vector.tensor_copy(b_plane[:], x_scales_b[:].indirect(list_b[:]))
+
+        wb_bf = held("wb_bf", [P, PASSES * N * 4], BF16)
+        wb_codes = held("wb_codes", [P, PASSES * N], U32)
+        wb_plane = held("wb_plane", [P, PASSES * N], U8)
+
+        def interleave(z):
+            nc.scalar.copy(
+                wb_bf[:].rearrange("p (b z c i j) -> p z b c j i", b=BLOCKS, z=PASSES, i=4, j=4)[:, z],
+                wb_raw[z][:].rearrange("p (j b c i) -> p b c j i", j=4, b=BLOCKS, i=4),
+            )
+
+        def quantize(b0, b1):
+            w0, w1 = b0 * PASSES * P, b1 * PASSES * P
+            nc.vector.quantize_mx(
+                out=wb_codes[:, w0:w1].bitcast(FP8X4),
+                scales=wb_plane[:, w0:w1],
+                in_=wb_bf[:, 4 * w0 : 4 * w1],
+            )
+
+        mm_banks = [psum.tile([P, BANK], F32, name="mm%d" % i) for i in range(2)]
+        turn_banks = [[psum.tile([P, BANK], F32, name="turn%d%d" % (i, h)) for h in range(HALVES)] for i in range(2)]
+        back_banks = [psum.tile([P, BANK], F32, name="back%d" % h) for h in range(HALVES)]
+
+        turn_of = [turn_banks[0], turn_banks[1], turn_banks[0], mm_banks]
+
+        p_sb = [held("p_sb%d" % b, [P, J], F32)[:] for b in range(BLOCKS)]
+        q_sb = [held("q_sb%d" % b, [P, J], F32) for b in range(BLOCKS)]
+        damp = [wb_raw[1 - b // 2][:, (b % 2) * T : (b % 2 + 1) * T] for b in range(BLOCKS)]
+        second = [held("second%d" % b, [P, T], F32) for b in range(BLOCKS)]
+
+        def product_p(b, bank):
+            for z in range(PASSES):
+                nc.tensor.matmul_mx(
+                    out=bank[:],
+                    lhsT=wa_codes[:, z, 2 * P * b : 2 * P * (b + 1)].bitcast(FP4X4),
+                    lhsT_scale=wa_plane[:, z, P * b : P * (b + 1)],
+                    rhs=a_words[z][:].bitcast(FP8X4),
+                    rhs_scale=a_plane[z][:],
+                    start=(z == 0),
+                    stop=(z == PASSES - 1),
+                )
+            nc.scalar.activation(p_sb[b], bank[:], ACT.Copy, scale=1.0 / RES_SCALE)
+
+        def product_q(b, bank):
+            for z in range(PASSES):
+                nc.tensor.matmul_mx(
+                    out=bank[:],
+                    lhsT=wb_codes[:, P * (PASSES * b + z) : P * (PASSES * b + z + 1)].bitcast(FP8X4),
+                    lhsT_scale=wb_plane[:, P * (PASSES * b + z) : P * (PASSES * b + z + 1)],
+                    rhs=b_words[z][:].bitcast(FP8X4),
+                    rhs_scale=b_plane[4 * z : P, :],
+                    start=(z == 0),
+                    stop=(z == PASSES - 1),
+                )
+            nc.scalar.activation(q_sb[b][:], bank[:], ACT.Copy, scale=1.0 / RES_SCALE)
+
+        def turn(b, src, first, last):
+            for h in range(HALVES):
+                for c in range(CHUNKS):
+                    col = h * BANK + c * P
+                    nc.tensor.matmul(
+                        turn_of[b][h][:, c * P : (c + 1) * P],
+                        lhsT=src[:, col : col + P],
+                        rhs=ident[:],
+                        is_transpose=True,
+                        start=(first and c == 0),
+                        stop=(last and c == CHUNKS - 1),
+                    )
+
+        def turn_back(b, h, bank):
+            turned = ring.tile([P, BANK], F32, name="turned")
+            nc.scalar.activation(turned[:], turn_of[b][h][:], ACT.Copy, scale=RES_SCALE)
+            for c in range(CHUNKS):
+                nc.tensor.transpose(bank[:, c * P : (c + 1) * P], turned[:, c * P : (c + 1) * P], ident[:])
+
+        def place_p(b):
+            win = p_win[b % 2]
+            nc.vector.tensor_copy(win[:].indirect(list_a[:]), p_sb[b])
+            nc.scalar.activation(damp[b], win[:], ACT.Abs)
+            nc.scalar.activation(damp[b], damp[b], ACT.Exp, scale=-RES_SCALE)
+            turn(b, win, True, False)
+            turn(b, res_sb[b], False, b == BLOCKS - 1)
+
+        def place_q(b):
+            win = q_win
+            nc.vector.tensor_tensor(win[:].indirect(list_b[:]), q_sb[b][:], gb_rows[:], ALU.mult)
+
+        def finish(b):
+            nc.vector.tensor_tensor(second[b][:], q_win[:], damp[b], ALU.mult)
+            turn(b, second[b], False, True)
+            for h in range(HALVES):
+                turn_back(b, h, back_banks[h])
+                done = held("done%d%d" % (b, h), [P, BANK], F32)
+                nc.scalar.copy(done[:], back_banks[h][:])
+                nc.scalar.dma_start(out[b * P : (b + 1) * P, h * BANK : (h + 1) * BANK], done[:])
+
+        def finish_last(b):
+            for h in range(HALVES):
+                cols = slice(h * BANK, (h + 1) * BANK)
+                nc.vector.tensor_tensor(second[b][:, cols], q_win[:, cols], damp[b][:, cols], ALU.mult)
+            for h in range(HALVES):
+                cols = slice(h * BANK, (h + 1) * BANK)
+                last = ring.tile([P, BANK], F32, name="last")
+                nc.vector.scalar_tensor_tensor(
+                    last[:], second[b][:, cols], RES_SCALE, mm_banks[h][:], ALU.mult, ALU.add
+                )
+                nc.sync.dma_start(out[b * P : (b + 1) * P, cols], last[:])
+
+        product_p(0, mm_banks[0])
+        product_p(1, mm_banks[1])
+        interleave(0)
+        interleave(1)
+        product_p(2, mm_banks[0])
+        product_p(3, mm_banks[1])
+        place_p(0)
+        place_p(1)
+        quantize(0, 1)
+        quantize(1, 2)
+        quantize(2, 4)
+        for b in range(BLOCKS):
+            product_q(b, mm_banks[b % 2])
+        place_q(0)
+        finish(0)
+        place_p(2)
+        place_p(3)
+        for h in range(HALVES):
+            turn_back(3, h, mm_banks[h])
+        place_q(1)
+        finish(1)
+        place_q(2)
+        finish(2)
+        place_q(3)
+        finish_last(3)

@@ -32,7 +32,6 @@ def tile_moe_second_choice_where_first_is_weak_kernel(
     nc = tc.nc
     with ExitStack() as ctx:
         keep = ctx.enter_context(tc.tile_pool(name="keep", bufs=1))
-        ring = ctx.enter_context(tc.tile_pool(name="ring", bufs=2))
         psum = ctx.enter_context(tc.psum_pool(name="psum", bufs=1))
 
         def held(name, shape, dtype):
@@ -41,65 +40,81 @@ def tile_moe_second_choice_where_first_is_weak_kernel(
         list_a = held("list_a", [P, J // 16], U16)
         list_b = held("list_b", [P, J // 16], U16)
         x_words = [held("x_words%d" % z, [P, T], U32) for z in range(PASSES)]
-        x_scales_a = held("x_scales_a", [P, PASSES, T], U8)
-        x_scales_b = held("x_scales_b", [P, T], U8)
+        x_scales = held("x_scales", [P, T], U8)
+        a_plane1 = held("a_plane1", [P, J], U8)
         wa_codes = held("wa_codes", [P, PASSES, 2 * N], U8)
         wa_plane = held("wa_plane", [P, PASSES, N], U8)
         wb_raw = [held("wb_raw%d" % z, [P, 4 * N], F32) for z in range(PASSES)]
         gb_rows = held("gb_rows", [P, J], F32)
         res_sb = [held("res%d" % b, [P, T], F32) for b in range(BLOCKS)]
         p_win = [held("p_win%d" % i, [P, T], F32) for i in range(2)]
-        q_win = held("q_win", [P, T], F32)
+        q_win = [held("q_win%d" % i, [P, T], F32) for i in range(2)]
         ident = held("ident", [P, P], F32)
 
-        nc.vector.memset(x_scales_a[:].rearrange("p z t -> p (z t)").bitcast(I32), 0)
-        nc.vector.memset(wa_plane[:].rearrange("p z n -> p (z n)").bitcast(I32), 0)
-        nc.vector.memset(x_scales_b[:].bitcast(I32), 0)
-        for win in p_win + [q_win]:
+        nc.gpsimd.memset(x_scales[:].bitcast(I32), 0)
+        nc.gpsimd.memset(wa_plane[:].rearrange("p z n -> p (z n)").bitcast(I32), 0)
+        nc.vector.memset(a_plane1[:].bitcast(I32), 0)
+        for win in p_win:
             nc.vector.memset(win[:], 0.0)
         make_identity(nc, ident[:])
+        for win in q_win:
+            nc.gpsimd.memset(win[:], 0.0)
 
         xs_i32 = xt_scales.bitcast(I32)
         was_i32 = wa_scales.bitcast(I32)
 
+        def load_words(z):
+            nc.sync.dma_start(x_words[z][:].bitcast(I32), xt_words[z].rearrange("p c r -> p (c r)").bitcast(I32))
+
+        def load_wb(z):
+            nc.sync.dma_start(wb_raw[z][:], wb[512 * z : 512 * (z + 1), :].rearrange("(p j) n -> p (j n)", j=4))
+
+        a_words = [held("a_words%d" % z, [P, J], U32) for z in range(PASSES)]
+        a_planes = held("a_planes", [P, J], U8)
+        b_words = [held("b_words%d" % z, [P, J], U32) for z in range(PASSES)]
+        b_plane = held("b_plane", [P, J], U8)
+
         nc.sync.dma_start(list_a[:], offs)
-        nc.sync.dma_start(x_words[0][:].bitcast(I32), xt_words[0].rearrange("p c r -> p (c r)").bitcast(I32))
-        nc.sync.dma_start(x_words[1][:].bitcast(I32), xt_words[1].rearrange("p c r -> p (c r)").bitcast(I32))
-        for r in range(4):
-            nc.sync.dma_start(
-                x_scales_a[r:P:32, :, :].bitcast(I32), xs_i32[:, r:16:4, :].rearrange("z q c -> q z c")
-            )
+        for q in range(4):
+            nc.sync.dma_start(x_scales[32 * q : 32 * q + 8, :].bitcast(I32), xs_i32[:, 4 * q : 4 * q + 4, :])
+        load_words(0)
+        load_words(1)
         nc.sync.dma_start(wa_codes[:].bitcast(I32), wa_words.bitcast(I32).rearrange("z p c -> p z c"))
         for r in range(4):
             nc.sync.dma_start(
                 wa_plane[r:P:32, :, :].bitcast(I32), was_i32[:, r:16:4, :].rearrange("z q c -> q z c")
             )
         nc.sync.dma_start(list_b[:], offs2)
+        nc.vector.tensor_copy(a_planes[:], x_scales[:].indirect(list_a[:]))
         for q in range(4):
-            nc.sync.dma_start(x_scales_b[32 * q : 32 * q + 8, :].bitcast(I32), xs_i32[:, 4 * q : 4 * q + 4, :])
-        for z in range(PASSES):
-            nc.sync.dma_start(wb_raw[z][:], wb[512 * z : 512 * (z + 1), :].rearrange("(p j) n -> p (j n)", j=4))
+            nc.sync.dma_start(
+                a_plane1[32 * q : 32 * q + 4, :].bitcast(I32), a_planes[32 * q + 4 : 32 * q + 8, :].bitcast(I32)
+            )
+        load_wb(0)
+        load_wb(1)
         nc.sync.dma_start(gb_rows[:], gb[0].partition_broadcast(P))
         for b in range(BLOCKS):
             nc.sync.dma_start(res_sb[b][:], res[b * P : (b + 1) * P, :])
 
-        a_words = [held("a_words%d" % z, [P, J], U32) for z in range(PASSES)]
-        a_plane = [held("a_plane%d" % z, [P, J], U8) for z in range(PASSES)]
-        b_words = [held("b_words%d" % z, [P, J], U32) for z in range(PASSES)]
-        b_plane = held("b_plane", [P, J], U8)
+        a_plane = [a_planes, a_plane1]
         for z in range(PASSES):
             nc.vector.tensor_copy(a_words[z][:], x_words[z][:].indirect(list_a[:]))
         for z in range(PASSES):
-            nc.vector.tensor_copy(a_plane[z][:], x_scales_a[:, z, :].indirect(list_a[:]))
-        for z in range(PASSES):
             nc.vector.tensor_copy(b_words[z][:], x_words[z][:].indirect(list_b[:]))
-        nc.vector.tensor_copy(b_plane[:], x_scales_b[:].indirect(list_b[:]))
+        nc.vector.tensor_copy(b_plane[:], x_scales[:].indirect(list_b[:]))
 
         wb_bf = held("wb_bf", [P, PASSES * N * 4], BF16)
         wb_codes = held("wb_codes", [P, PASSES * N], U32)
         wb_plane = held("wb_plane", [P, PASSES * N], U8)
 
-        def interleave(z):
+        def interleave_on_gpsimd(z):
+            nc.gpsimd.tensor_scalar(
+                wb_bf[:].rearrange("p (b z n j) -> p z b n j", b=BLOCKS, z=PASSES, j=4)[:, z],
+                wb_raw[z][:].rearrange("p (j b n) -> p b n j", j=4, b=BLOCKS),
+                1.0, 0.0, ALU.mult, ALU.add,
+            )
+
+        def interleave_on_scalar(z):
             nc.scalar.copy(
                 wb_bf[:].rearrange("p (b z c i j) -> p z b c j i", b=BLOCKS, z=PASSES, i=4, j=4)[:, z],
                 wb_raw[z][:].rearrange("p (j b c i) -> p b c j i", j=4, b=BLOCKS, i=4),
@@ -114,15 +129,25 @@ def tile_moe_second_choice_where_first_is_weak_kernel(
             )
 
         mm_banks = [psum.tile([P, BANK], F32, name="mm%d" % i) for i in range(2)]
-        turn_banks = [[psum.tile([P, BANK], F32, name="turn%d%d" % (i, h)) for h in range(HALVES)] for i in range(2)]
+        turn_banks = [psum.tile([P, BANK], F32, name="turn%d" % i) for i in range(4)]
         back_banks = [psum.tile([P, BANK], F32, name="back%d" % h) for h in range(HALVES)]
 
-        turn_of = [turn_banks[0], turn_banks[1], turn_banks[0], mm_banks]
+        turn_of = [turn_banks[0:2], mm_banks, [turn_banks[2], turn_banks[0]]]
 
         p_sb = [held("p_sb%d" % b, [P, J], F32)[:] for b in range(BLOCKS)]
-        q_sb = [held("q_sb%d" % b, [P, J], F32) for b in range(BLOCKS)]
-        damp = [wb_raw[1 - b // 2][:, (b % 2) * T : (b % 2 + 1) * T] for b in range(BLOCKS)]
-        second = [held("second%d" % b, [P, T], F32) for b in range(BLOCKS)]
+        q_all = held("q_all", [P, BLOCKS * J], F32)
+        q_sb = [q_all[:, b * J : (b + 1) * J] for b in range(BLOCKS)]
+        qw_sb = [held("qw_sb%d" % b, [P, J], F32)[:] for b in range(BLOCKS)]
+        damp = [wb_raw[1][:, 0:T], wb_raw[0][:, 0:T], wb_raw[1][:, T : 2 * T]]
+        first_sum = damp[2]
+        q_win_of = [q_win[0], q_win[1], q_win[0], q_win[0]]
+        p_win_of = [p_win[0], p_win[0], p_win[1], p_win[1]]
+        turned = [held("turned%d" % b, [P, T], F32) for b in range(BLOCKS - 1)]
+        damp.append(turned[1][:])
+        second = [q_all[:, 2 * J : 4 * J]]
+        second.append(second[0])
+        second.append(turned[0][:])
+        second.append(held("second3", [P, T], F32)[:])
 
         def product_p(b, bank):
             for z in range(PASSES):
@@ -148,10 +173,13 @@ def tile_moe_second_choice_where_first_is_weak_kernel(
                     start=(z == 0),
                     stop=(z == PASSES - 1),
                 )
-            nc.scalar.activation(q_sb[b][:], bank[:], ACT.Copy, scale=1.0 / RES_SCALE)
+            nc.scalar.activation(q_sb[b], bank[:], ACT.Copy, scale=1.0 / RES_SCALE)
 
-        def turn(b, src, first, last):
-            for h in range(HALVES):
+        def gate(b):
+            nc.gpsimd.tensor_tensor(qw_sb[b], q_sb[b], gb_rows[:], ALU.mult)
+
+        def turn(b, src, first, last, halves=range(HALVES)):
+            for h in halves:
                 for c in range(CHUNKS):
                     col = h * BANK + c * P
                     nc.tensor.matmul(
@@ -163,67 +191,98 @@ def tile_moe_second_choice_where_first_is_weak_kernel(
                         stop=(last and c == CHUNKS - 1),
                     )
 
-        def turn_back(b, h, bank):
-            turned = ring.tile([P, BANK], F32, name="turned")
-            nc.scalar.activation(turned[:], turn_of[b][h][:], ACT.Copy, scale=RES_SCALE)
-            for c in range(CHUNKS):
-                nc.tensor.transpose(bank[:, c * P : (c + 1) * P], turned[:, c * P : (c + 1) * P], ident[:])
-
         def place_p(b):
-            win = p_win[b % 2]
-            nc.vector.tensor_copy(win[:].indirect(list_a[:]), p_sb[b])
-            nc.scalar.activation(damp[b], win[:], ACT.Abs)
-            nc.scalar.activation(damp[b], damp[b], ACT.Exp, scale=-RES_SCALE)
-            turn(b, win, True, False)
-            turn(b, res_sb[b], False, b == BLOCKS - 1)
+            nc.vector.tensor_copy(p_win_of[b][:].indirect(list_a[:]), p_sb[b])
+
+        def damping(b, step=T):
+            for c0 in range(0, T, step):
+                nc.scalar.activation(damp[b][:, c0 : c0 + step], p_win_of[b][:, c0 : c0 + step], ACT.Abs)
+            for c0 in range(0, T, step):
+                part = damp[b][:, c0 : c0 + step]
+                nc.scalar.activation(part, part, ACT.Exp, scale=-RES_SCALE)
 
         def place_q(b):
-            win = q_win
-            nc.vector.tensor_tensor(win[:].indirect(list_b[:]), q_sb[b][:], gb_rows[:], ALU.mult)
+            nc.vector.tensor_copy(q_win_of[b][:].indirect(list_b[:]), qw_sb[b])
 
-        def finish(b):
-            nc.vector.tensor_tensor(second[b][:], q_win[:], damp[b], ALU.mult)
+        def weigh(b):
+            nc.gpsimd.tensor_tensor(second[b], q_win_of[b][:], damp[b], ALU.mult)
+
+        def close_sum(b):
             turn(b, second[b], False, True)
             for h in range(HALVES):
-                turn_back(b, h, back_banks[h])
+                nc.scalar.activation(
+                    turned[b][:, h * BANK : (h + 1) * BANK], turn_of[b][h][:], ACT.Copy, scale=RES_SCALE
+                )
+
+        def turn_back(b):
+            for h in range(HALVES):
+                for c in range(CHUNKS):
+                    col = h * BANK + c * P
+                    nc.tensor.transpose(back_banks[h][:, c * P : (c + 1) * P], turned[b][:, col : col + P], ident[:])
+
+        def store(b, queue):
+            for h in range(HALVES):
                 done = held("done%d%d" % (b, h), [P, BANK], F32)
                 nc.scalar.copy(done[:], back_banks[h][:])
-                nc.scalar.dma_start(out[b * P : (b + 1) * P, h * BANK : (h + 1) * BANK], done[:])
+                queue.dma_start(out[b * P : (b + 1) * P, h * BANK : (h + 1) * BANK], done[:])
 
         def finish_last(b):
             for h in range(HALVES):
                 cols = slice(h * BANK, (h + 1) * BANK)
-                nc.vector.tensor_tensor(second[b][:, cols], q_win[:, cols], damp[b][:, cols], ALU.mult)
-            for h in range(HALVES):
-                cols = slice(h * BANK, (h + 1) * BANK)
-                last = ring.tile([P, BANK], F32, name="last")
                 nc.vector.scalar_tensor_tensor(
-                    last[:], second[b][:, cols], RES_SCALE, mm_banks[h][:], ALU.mult, ALU.add
+                    second[b][:, cols], q_win_of[b][:, cols], RES_SCALE, damp[b][:, cols], ALU.mult, ALU.mult
                 )
-                nc.sync.dma_start(out[b * P : (b + 1) * P, cols], last[:])
+            for c0, c1 in ((0, 512), (512, 768), (768, 1024)):
+                last = held("last%d" % c0, [P, c1 - c0], F32)
+                nc.vector.scalar_tensor_tensor(
+                    last[:], first_sum[:, c0:c1], RES_SCALE, second[b][:, c0:c1], ALU.mult, ALU.add
+                )
+                nc.sync.dma_start(out[b * P : (b + 1) * P, c0:c1], last[:])
 
-        product_p(0, mm_banks[0])
-        product_p(1, mm_banks[1])
-        interleave(0)
-        interleave(1)
-        product_p(2, mm_banks[0])
-        product_p(3, mm_banks[1])
+        p_banks = mm_banks + back_banks
+        q_banks = turn_banks[2:4] + mm_banks
+        for b in (0, 2, 1, 3):
+            product_p(b, p_banks[b])
+        interleave_on_gpsimd(0)
+        interleave_on_scalar(1)
         place_p(0)
-        place_p(1)
+        damping(0)
+        turn(0, p_win_of[0], True, False)
+        place_p(2)
         quantize(0, 1)
         quantize(1, 2)
         quantize(2, 4)
         for b in range(BLOCKS):
-            product_q(b, mm_banks[b % 2])
+            product_q(b, q_banks[b])
+        for b in range(BLOCKS):
+            gate(b)
+        damping(2)
+        turn(0, res_sb[0], False, False)
+        place_p(1)
+        damping(1)
+        turn(1, p_win_of[1], True, False)
+        turn(1, res_sb[1], False, False)
+        turn(2, p_win_of[2], True, False, [0])
+        turn(2, res_sb[2], False, False, [0])
         place_q(0)
-        finish(0)
-        place_p(2)
-        place_p(3)
-        for h in range(HALVES):
-            turn_back(3, h, mm_banks[h])
+        weigh(0)
+        close_sum(0)
+        turn(2, p_win_of[2], True, False, [1])
+        turn_back(0)
+        store(0, nc.sync)
         place_q(1)
-        finish(1)
+        weigh(1)
+        close_sum(1)
+        turn_back(1)
+        store(1, nc.sync)
+        turn(2, res_sb[2], False, False, [1])
         place_q(2)
-        finish(2)
+        weigh(2)
+        place_p(3)
+        damping(3, BANK)
+        nc.gpsimd.tensor_tensor(first_sum[:], p_win_of[3][:], res_sb[3][:], ALU.add)
+        close_sum(2)
+        turn_back(2)
+        store(2, nc.scalar)
         place_q(3)
         finish_last(3)

@@ -53,11 +53,9 @@ def tile_moe_second_choice_where_first_is_weak_kernel(
 
         nc.gpsimd.memset(x_scales[:].bitcast(I32), 0)
         nc.gpsimd.memset(wa_plane[:].rearrange("p z n -> p (z n)").bitcast(I32), 0)
-        nc.vector.memset(a_plane1[:].bitcast(I32), 0)
-        for win in p_win:
-            nc.vector.memset(win[:], 0.0)
+        nc.gpsimd.memset(a_plane1[:].bitcast(I32), 0)
         make_identity(nc, ident[:])
-        for win in q_win:
+        for win in p_win + q_win:
             nc.gpsimd.memset(win[:], 0.0)
 
         xs_i32 = xt_scales.bitcast(I32)
@@ -92,8 +90,9 @@ def tile_moe_second_choice_where_first_is_weak_kernel(
             )
         load_wb(0)
         load_wb(1)
+        nc.sync.dma_start(res_sb[0][:], res[0:P, :])
         nc.sync.dma_start(gb_rows[:], gb[0].partition_broadcast(P))
-        for b in range(BLOCKS):
+        for b in (2, 1, 3):
             nc.sync.dma_start(res_sb[b][:], res[b * P : (b + 1) * P, :])
 
         a_plane = [a_planes, a_plane1]
@@ -204,12 +203,14 @@ def tile_moe_second_choice_where_first_is_weak_kernel(
         def place_q(b):
             nc.vector.tensor_copy(q_win_of[b][:].indirect(list_b[:]), qw_sb[b])
 
-        def weigh(b):
-            nc.gpsimd.tensor_tensor(second[b], q_win_of[b][:], damp[b], ALU.mult)
+        def weigh(b, step=T):
+            for c0 in range(0, T, step):
+                cols = slice(c0, c0 + step)
+                nc.gpsimd.tensor_tensor(second[b][:, cols], q_win_of[b][:, cols], damp[b][:, cols], ALU.mult)
 
-        def close_sum(b):
-            turn(b, second[b], False, True)
-            for h in range(HALVES):
+        def close_sum(b, halves=range(HALVES)):
+            turn(b, second[b], False, True, halves)
+            for h in halves:
                 nc.scalar.activation(
                     turned[b][:, h * BANK : (h + 1) * BANK], turn_of[b][h][:], ACT.Copy, scale=RES_SCALE
                 )
@@ -277,11 +278,12 @@ def tile_moe_second_choice_where_first_is_weak_kernel(
         store(1, nc.sync)
         turn(2, res_sb[2], False, False, [1])
         place_q(2)
-        weigh(2)
+        weigh(2, BANK)
+        close_sum(2, [0])
         place_p(3)
         damping(3, BANK)
         nc.gpsimd.tensor_tensor(first_sum[:], p_win_of[3][:], res_sb[3][:], ALU.add)
-        close_sum(2)
+        close_sum(2, [1])
         turn_back(2)
         store(2, nc.scalar)
         place_q(3)

from contextlib import ExitStack

import concourse.mybir as mybir
from concourse.masks import make_identity

K, T, J, N = 1024, 1024, 512, 512
FLOPS = 2 * 2 * K * J * N

F32 = mybir.dt.float32
BF16 = mybir.dt.bfloat16
I32 = mybir.dt.int32
U32 = mybir.dt.uint32
U16 = mybir.dt.uint16
U8 = mybir.dt.uint8
FP8X4 = mybir.dt.float8_e4m3fn_x4
FP4X4 = mybir.dt.float4_e2m1fn_x4
ACT = mybir.ActivationFunctionType
ALU = mybir.AluOpType

P = 128
PASSES = K // 512
BLOCKS = N // P
BANK = 512
HALVES = T // BANK
CHUNKS = BANK // P
RES_SCALE = 0.3


def tile_moe_second_choice_where_first_is_weak_kernel(
    tc, xt_words, xt_scales, wa_words, wa_scales, wb, gb, res, offs, offs2, out
):
    nc = tc.nc
    with ExitStack() as ctx:
        keep = ctx.enter_context(tc.tile_pool(name="keep", bufs=1))
        psum = ctx.enter_context(tc.psum_pool(name="psum", bufs=1))

        def held(name, shape, dtype):
            return keep.tile(shape, dtype, name=name, align_bytes=64)

        list_a = held("list_a", [P, J // 16], U16)
        list_b = held("list_b", [P, J // 16], U16)
        x_words = [held("x_words%d" % z, [P, T], U32) for z in range(PASSES)]
        x_scales = held("x_scales", [P, T], U8)
        a_plane1 = held("a_plane1", [P, J], U8)
        wa_codes = held("wa_codes", [P, PASSES, 2 * N], U8)
        wa_plane = held("wa_plane", [P, PASSES, N], U8)
        wb_raw = [held("wb_raw%d" % z, [P, 4 * N], F32) for z in range(PASSES)]
        gb_rows = held("gb_rows", [P, J], F32)
        res_sb = [held("res%d" % b, [P, T], F32) for b in range(BLOCKS)]
        p_win = [held("p_win%d" % i, [P, T], F32) for i in range(2)]
        q_win = [held("q_win%d" % i, [P, T], F32) for i in range(2)]
        ident = held("ident", [P, P], F32)

        nc.gpsimd.memset(x_scales[:].bitcast(I32), 0)
        nc.gpsimd.memset(wa_plane[:].rearrange("p z n -> p (z n)").bitcast(I32), 0)
        nc.gpsimd.memset(a_plane1[:].bitcast(I32), 0)
        make_identity(nc, ident[:])
        for win in p_win + q_win:
            nc.gpsimd.memset(win[:], 0.0)

        xs_i32 = xt_scales.bitcast(I32)
        was_i32 = wa_scales.bitcast(I32)

        def load_words(z):
            nc.sync.dma_start(x_words[z][:].bitcast(I32), xt_words[z].rearrange("p c r -> p (c r)").bitcast(I32))

        def load_wb(z):
            nc.sync.dma_start(wb_raw[z][:], wb[512 * z : 512 * (z + 1), :].rearrange("(p j) n -> p (j n)", j=4))

        a_words = [held("a_words%d" % z, [P, J], U32) for z in range(PASSES)]
        a_planes = held("a_planes", [P, J], U8)
        b_words = [held("b_words%d" % z, [P, J], U32) for z in range(PASSES)]
        b_plane = held("b_plane", [P, J], U8)

        nc.sync.dma_start(list_a[:], offs)
        for q in range(4):
            nc.sync.dma_start(x_scales[32 * q : 32 * q + 8, :].bitcast(I32), xs_i32[:, 4 * q : 4 * q + 4, :])
        load_words(0)
        load_words(1)
        nc.sync.dma_start(wa_codes[:].bitcast(I32), wa_words.bitcast(I32).rearrange("z p c -> p z c"))
        for r in range(4):
            nc.sync.dma_start(
                wa_plane[r:P:32, :, :].bitcast(I32), was_i32[:, r:16:4, :].rearrange("z q c -> q z c")
            )
        nc.sync.dma_start(list_b[:], offs2)
        nc.vector.tensor_copy(a_planes[:], x_scales[:].indirect(list_a[:]))
        for q in range(4):
            nc.sync.dma_start(
                a_plane1[32 * q : 32 * q + 4, :].bitcast(I32), a_planes[32 * q + 4 : 32 * q + 8, :].bitcast(I32)
            )
        load_wb(0)
        load_wb(1)
        nc.sync.dma_start(res_sb[0][:], res[0:P, :])
        nc.sync.dma_start(gb_rows[:], gb[0].partition_broadcast(P))
        for b in (2, 1, 3):
            nc.sync.dma_start(res_sb[b][:], res[b * P : (b + 1) * P, :])

        a_plane = [a_planes, a_plane1]
        for z in range(PASSES):
            nc.vector.tensor_copy(a_words[z][:], x_words[z][:].indirect(list_a[:]))
        for z in range(PASSES):
            nc.vector.tensor_copy(b_words[z][:], x_words[z][:].indirect(list_b[:]))
        nc.vector.tensor_copy(b_plane[:], x_scales[:].indirect(list_b[:]))

        wb_bf = held("wb_bf", [P, PASSES * N * 4], BF16)
        wb_codes = held("wb_codes", [P, PASSES * N], U32)
        wb_plane = held("wb_plane", [P, PASSES * N], U8)

        def interleave_on_gpsimd(z):
            nc.gpsimd.tensor_scalar(
                wb_bf[:].rearrange("p (b z n j) -> p z b n j", b=BLOCKS, z=PASSES, j=4)[:, z],
                wb_raw[z][:].rearrange("p (j b n) -> p b n j", j=4, b=BLOCKS),
                1.0, 0.0, ALU.mult, ALU.add,
            )

        def interleave_on_scalar(z):
            nc.scalar.copy(
                wb_bf[:].rearrange("p (b z c i j) -> p z b c j i", b=BLOCKS, z=PASSES, i=4, j=4)[:, z],
                wb_raw[z][:].rearrange("p (j b c i) -> p b c j i", j=4, b=BLOCKS, i=4),
            )

        def quantize(b0, b1):
            w0, w1 = b0 * PASSES * P, b1 * PASSES * P
            nc.vector.quantize_mx(
                out=wb_codes[:, w0:w1].bitcast(FP8X4),
                scales=wb_plane[:, w0:w1],
                in_=wb_bf[:, 4 * w0 : 4 * w1],
            )

        mm_banks = [psum.tile([P, BANK], F32, name="mm%d" % i) for i in range(2)]
        turn_banks = [psum.tile([P, BANK], F32, name="turn%d" % i) for i in range(4)]
        back_banks = [psum.tile([P, BANK], F32, name="back%d" % h) for h in range(HALVES)]

        turn_of = [turn_banks[0:2], mm_banks, [turn_banks[2], turn_banks[0]]]

        p_sb = [held("p_sb%d" % b, [P, J], F32)[:] for b in range(BLOCKS)]
        q_all = held("q_all", [P, BLOCKS * J], F32)
        q_sb = [q_all[:, b * J : (b + 1) * J] for b in range(BLOCKS)]
        qw_sb = [held("qw_sb%d" % b, [P, J], F32)[:] for b in range(BLOCKS)]
        damp = [wb_raw[1][:, 0:T], wb_raw[0][:, 0:T], wb_raw[1][:, T : 2 * T]]
        first_sum = damp[2]
        q_win_of = [q_win[0], q_win[1], q_win[0], q_win[0]]
        p_win_of = [p_win[0], p_win[0], p_win[1], p_win[1]]
        turned = [held("turned%d" % b, [P, T], F32) for b in range(BLOCKS - 1)]
        damp.append(turned[1][:])
        second = [q_all[:, 2 * J : 4 * J]]
        second.append(second[0])
        second.append(turned[0][:])
        second.append(held("second3", [P, T], F32)[:])

        def product_p(b, bank):
            for z in range(PASSES):
                nc.tensor.matmul_mx(
                    out=bank[:],
                    lhsT=wa_codes[:, z, 2 * P * b : 2 * P * (b + 1)].bitcast(FP4X4),
                    lhsT_scale=wa_plane[:, z, P * b : P * (b + 1)],
                    rhs=a_words[z][:].bitcast(FP8X4),
                    rhs_scale=a_plane[z][:],
                    start=(z == 0),
                    stop=(z == PASSES - 1),
                )
            nc.scalar.activation(p_sb[b], bank[:], ACT.Copy, scale=1.0 / RES_SCALE)

        def product_q(b, bank):
            for z in range(PASSES):
                nc.tensor.matmul_mx(
                    out=bank[:],
                    lhsT=wb_codes[:, P * (PASSES * b + z) : P * (PASSES * b + z + 1)].bitcast(FP8X4),
                    lhsT_scale=wb_plane[:, P * (PASSES * b + z) : P * (PASSES * b + z + 1)],
                    rhs=b_words[z][:].bitcast(FP8X4),
                    rhs_scale=b_plane[4 * z : P, :],
                    start=(z == 0),
                    stop=(z == PASSES - 1),
                )
            nc.scalar.activation(q_sb[b], bank[:], ACT.Copy, scale=1.0 / RES_SCALE)

        def gate(b):
            nc.gpsimd.tensor_tensor(qw_sb[b], q_sb[b], gb_rows[:], ALU.mult)

        def turn(b, src, first, last, halves=range(HALVES)):
            for h in halves:
                for c in range(CHUNKS):
                    col = h * BANK + c * P
                    nc.tensor.matmul(
                        turn_of[b][h][:, c * P : (c + 1) * P],
                        lhsT=src[:, col : col + P],
                        rhs=ident[:],
                        is_transpose=True,
                        start=(first and c == 0),
                        stop=(last and c == CHUNKS - 1),
                    )

        def place_p(b):
            nc.vector.tensor_copy(p_win_of[b][:].indirect(list_a[:]), p_sb[b])

        def damping(b, step=T):
            for c0 in range(0, T, step):
                nc.scalar.activation(damp[b][:, c0 : c0 + step], p_win_of[b][:, c0 : c0 + step], ACT.Abs)
            for c0 in range(0, T, step):
                part = damp[b][:, c0 : c0 + step]
                nc.scalar.activation(part, part, ACT.Exp, scale=-RES_SCALE)

        def place_q(b):
            nc.vector.tensor_copy(q_win_of[b][:].indirect(list_b[:]), qw_sb[b])

        def weigh(b, step=T):
            for c0 in range(0, T, step):
                cols = slice(c0, c0 + step)
                nc.gpsimd.tensor_tensor(second[b][:, cols], q_win_of[b][:, cols], damp[b][:, cols], ALU.mult)

        def close_sum(b, halves=range(HALVES)):
            turn(b, second[b], False, True, halves)
            for h in halves:
                nc.scalar.activation(
                    turned[b][:, h * BANK : (h + 1) * BANK], turn_of[b][h][:], ACT.Copy, scale=RES_SCALE
                )

        def turn_back(b):
            for h in range(HALVES):
                for c in range(CHUNKS):
                    col = h * BANK + c * P
                    nc.tensor.transpose(back_banks[h][:, c * P : (c + 1) * P], turned[b][:, col : col + P], ident[:])

        def store(b, queue):
            for h in range(HALVES):
                done = held("done%d%d" % (b, h), [P, BANK], F32)
                nc.scalar.copy(done[:], back_banks[h][:])
                queue.dma_start(out[b * P : (b + 1) * P, h * BANK : (h + 1) * BANK], done[:])

        def finish_last(b):
            for h in range(HALVES):
                cols = slice(h * BANK, (h + 1) * BANK)
                nc.vector.scalar_tensor_tensor(
                    second[b][:, cols], q_win_of[b][:, cols], RES_SCALE, damp[b][:, cols], ALU.mult, ALU.mult
                )
            for c0, c1 in ((0, 512), (512, 768), (768, 1024)):
                last = held("last%d" % c0, [P, c1 - c0], F32)
                nc.vector.scalar_tensor_tensor(
                    last[:], first_sum[:, c0:c1], RES_SCALE, second[b][:, c0:c1], ALU.mult, ALU.add
                )
                nc.sync.dma_start(out[b * P : (b + 1) * P, c0:c1], last[:])

        p_banks = mm_banks + back_banks
        q_banks = turn_banks[2:4] + mm_banks
        for b in (0, 2, 1, 3):
            product_p(b, p_banks[b])
        interleave_on_gpsimd(0)
        interleave_on_scalar(1)
        place_p(0)
        damping(0)
        turn(0, p_win_of[0], True, False)
        place_p(2)
        quantize(0, 1)
        quantize(1, 2)
        quantize(2, 4)
        for b in range(BLOCKS):
            product_q(b, q_banks[b])
        for b in range(BLOCKS):
            gate(b)
        damping(2)
        turn(0, res_sb[0], False, False)
        place_p(1)
        damping(1)
        turn(1, p_win_of[1], True, False)
        turn(1, res_sb[1], False, False)
        turn(2, p_win_of[2], True, False, [0])
        turn(2, res_sb[2], False, False, [0])
        place_q(0)
        weigh(0)
        close_sum(0)
        turn(2, p_win_of[2], True, False, [1])
        turn_back(0)
        store(0, nc.sync)
        place_q(1)
        weigh(1)
        close_sum(1)
        turn_back(1)
        store(1, nc.sync)
        turn(2, res_sb[2], False, False, [1])
        place_q(2)
        weigh(2, BANK)
        close_sum(2, [0])
        place_p(3)
        damping(3, BANK)
        nc.gpsimd.tensor_tensor(first_sum[:], p_win_of[3][:], res_sb[3][:], ALU.add)
        close_sum(2, [1])
        turn_back(2)
        store(2, nc.scalar)
        place_q(3)
        finish_last(3)
